import numpy as np
import ml_dtypes


def mxq(x, axis, fmt="e4m3"):
    dtype, down = {"e4m3": (ml_dtypes.float8_e4m3fn, 7), "e5m2": (ml_dtypes.float8_e5m2, 14)}[fmt]
    v = np.moveaxis(np.asarray(x, np.float32).astype(ml_dtypes.bfloat16).astype(np.float64), axis, -1)
    blocks = v.reshape(v.shape[:-1] + (-1, 32))
    amax = np.abs(blocks).max(-1, keepdims=True)
    byte = np.maximum(np.where(amax > 0, np.frexp(amax)[1] - 1 + 127, 0) - down, 1)
    scale = np.exp2(byte - 127.0)
    codes = (blocks / scale).astype(np.float32).astype(dtype).astype(np.float64)
    return np.moveaxis((codes * scale).reshape(v.shape), -1, axis)


WIDE = False


def mx_kscale(k):
    if not WIDE:
        return np.ones(k)
    levels = np.array([10, -10, 5, -5, 0])
    if k % 512:
        return np.exp2(np.random.permutation(np.resize(levels, k // 32))).repeat(32)
    a = np.empty((k // 512, 16))
    for p in range(k // 512):
        a[p, :8] = np.random.permutation(np.resize(levels, 8))
        for g in range(8):
            far = levels[np.abs(levels - a[p, g]) >= 10]
            a[p, g + 8] = far[np.random.randint(len(far))]
    return np.exp2(a.ravel()).repeat(32)


BF16 = ml_dtypes.bfloat16


def bf(x):
    return np.asarray(x, np.float32).astype(BF16)


def f64(x):
    return np.asarray(x).astype(np.float64)


E2M1 = np.array([0.0, 0.5, 1.0, 1.5, 2.0, 3.0, 4.0, 6.0, -0.0, -0.5, -1.0, -1.5, -2.0, -3.0, -4.0, -6.0])


def pack_weight(w, fmt):
    k, n = w.shape
    w = f64(bf(w)).reshape(k // 32, 32, n)
    amax = np.abs(w).max(1)
    if fmt == "e4m3":
        byte = np.frexp(amax)[1] - 1 + 127 - 7
    else:
        mant, ex = np.frexp(amax / 6.0)
        byte = np.where(mant > 0.5, ex, ex - 1) + 127
    byte = np.clip(np.where(amax > 0, byte, 1), 1, 254)
    scaled = (w * np.exp2(127.0 - byte)[:, None, :]).reshape(k, n).astype(np.float32)
    by_word = np.ascontiguousarray(scaled.reshape(k // 512, 128, 4, n).transpose(0, 1, 3, 2))
    if fmt == "e4m3":
        words = by_word.astype(ml_dtypes.float8_e4m3fn).view(np.uint8)
    else:
        c = by_word.astype(ml_dtypes.float4_e2m1fn).view(np.uint8) & 0xF
        words = c[..., 0::2] | (c[..., 1::2] << 4)
    return np.ascontiguousarray(words), np.ascontiguousarray(byte.astype(np.uint8).reshape(k // 512, 16, n))


def unpack_weight(words, scales, fmt):
    g, p, n, _ = words.shape
    if fmt == "e4m3":
        vals = np.ascontiguousarray(words).view(ml_dtypes.float8_e4m3fn).astype(np.float64)
    else:
        nib = np.empty((g, p, n, 4), np.uint8)
        nib[..., 0::2] = words & 0xF
        nib[..., 1::2] = words >> 4
        vals = E2M1[nib]
    vals = vals * np.repeat(np.exp2(scales.astype(np.float64) - 127.0), 8, axis=1)[..., None]
    return vals.transpose(0, 1, 3, 2).reshape(g * 512, n)
def pack4(w):
    words, scales = pack_weight(w, "e2m1")
    return words.reshape(words.shape[0], 128, -1), scales


def unpack4(words, scales):
    return unpack_weight(words.reshape(words.shape[0], 128, -1, 2), scales, "e2m1")


def planes(Y):
    n, m = Y.shape
    b = f64(bf(Y)).reshape(n // 32, 32, m)
    amax = np.abs(b).max(1)
    byte = np.clip(np.where(amax > 0, np.frexp(amax)[1] - 1 + 127 - 7, 1), 1, 254)
    codes = (b * np.exp2(127.0 - byte)[:, None, :]).reshape(n, m).astype(np.float32).astype(ml_dtypes.float8_e4m3fn).view(np.uint8)
    words = codes.reshape(n // 512, 128, 4, m).transpose(0, 1, 3, 2)
    return np.ascontiguousarray(words), np.ascontiguousarray(byte.astype(np.uint8).reshape(n // 512, 16, m))


R, D, P, Q = 1024, 1024, 512, 1024


def centered_bins(logits, gain):
    bins = logits.shape[-1]
    e = np.exp(logits - logits.max(-1, keepdims=True))
    probs = e / e.sum(-1, keepdims=True)
    return (bins * probs - 1.0) * gain


def setup_inputs():
    s, tx, ty = mx_kscale(D), mx_kscale(P), mx_kscale(Q)
    h = bf(np.random.standard_normal((R, D)) * s)
    wx_words, wx_scales = pack4(np.random.standard_normal((D, P)) / np.sqrt(D) / s[:, None])
    wy_words, wy_scales = pack4(np.random.standard_normal((D, Q)) / np.sqrt(D) / s[:, None])
    gx = bf((1.0 + 0.1 * np.random.standard_normal(P)) * tx)
    gy = bf((1.0 + 0.1 * np.random.standard_normal(Q)) * ty)
    ex_words, ex_scales = pack4(np.random.standard_normal((P, D)) / np.sqrt(P) / tx[:, None])
    ey_words, ey_scales = pack4(np.random.standard_normal((Q, D)) / np.sqrt(Q) / ty[:, None])
    return {
        "h": h,
        "wx_words": wx_words,
        "wx_scales": wx_scales,
        "wy_words": wy_words,
        "wy_scales": wy_scales,
        "gx": gx,
        "gy": gy,
        "ex_words": ex_words,
        "ex_scales": ex_scales,
        "ey_words": ey_words,
        "ey_scales": ey_scales,
    }


def core(h, wx_words, wx_scales, wy_words, wy_scales, gx, gy, ex_words, ex_scales, ey_words, ey_scales):
    hq = mxq(f64(h), 1, "e4m3")
    lx = hq @ unpack4(wx_words, wx_scales)
    ly = hq @ unpack4(wy_words, wy_scales)
    cx = centered_bins(lx, f64(gx))
    cy = centered_bins(ly, f64(gy))
    y = (mxq(cx, 1, "e4m3") @ unpack4(ex_words, ex_scales)) + (mxq(cy, 1, "e4m3") @ unpack4(ey_words, ey_scales))
    return y


def reference(h, wx_words, wx_scales, wy_words, wy_scales, gx, gy, ex_words, ex_scales, ey_words, ey_scales):
    R_out = core(h, wx_words, wx_scales, wy_words, wy_scales, gx, gy, ex_words, ex_scales, ey_words, ey_scales)
    words, scales = planes(R_out)
    return R_out, words, scales

@@ -1,0 +1,348 @@
+from contextlib import ExitStack
+
+import concourse.mybir as mybir
+from concourse.masks import make_identity
+
+R, D, BX, BY = 1024, 1024, 512, 1024
+FLOPS = 2 * R * D * (BX + BY) * 2
+
+F32 = mybir.dt.float32
+BF16 = mybir.dt.bfloat16
+I32 = mybir.dt.int32
+U32 = mybir.dt.uint32
+U8 = mybir.dt.uint8
+FP8X4 = mybir.dt.float8_e4m3fn_x4
+FP4X4 = mybir.dt.float4_e2m1fn_x4
+ALU = mybir.AluOpType
+ACT = mybir.ActivationFunctionType
+AX = mybir.AxisListType
+
+P = 128
+PACK = 4
+BANK = 512
+TILES = R // P
+KP = D // BANK
+NB = (BX + BY) // BANK
+LOWEST = -3.0e38
+
+
+def tile_simccsoftcoordinatereembedding_x2_kernel(
+    tc, h, wx_words, wx_scales, wy_words, wy_scales, gx, gy, ex_words, ex_scales, ey_words, ey_scales, out_0, out_1, out_2
+):
+    nc = tc.nc
+    with ExitStack() as ctx:
+        sb = ctx.enter_context(tc.tile_pool(name="sb", bufs=1))
+        ps = ctx.enter_context(tc.psum_pool(name="ps", bufs=1))
+        ctx.enter_context(tc.manual_schedule())
+
+        def tiles(name, count, shape, dtype):
+            return [sb.tile(shape, dtype, name="%s%d" % (name, n), align_bytes=64) for n in range(count)]
+
+        banks = [ps.tile([P, BANK], F32, name="bank%d" % n) for n in range(8)]
+        ident = sb.tile([P, P], F32, name="ident", align_bytes=64)
+        warm = sb.tile([P, 8], F32, name="warm", align_bytes=64)
+        warm2 = sb.tile([P, 8], F32, name="warm2", align_bytes=64)
+        wxw = sb.tile([P, KP, 2 * BX], U8, name="wxw", align_bytes=64)
+        wyw = sb.tile([P, KP, 2 * BY], U8, name="wyw", align_bytes=64)
+        wxs = sb.tile([P, KP, BX], U8, name="wxs", align_bytes=64)
+        wys = sb.tile([P, KP, BY], U8, name="wys", align_bytes=64)
+        exw = sb.tile([P, 1, 2 * D], U8, name="exw", align_bytes=64)
+        eyw = sb.tile([P, 2, 2 * D], U8, name="eyw", align_bytes=64)
+        exs = sb.tile([P, 1, D], U8, name="exs", align_bytes=64)
+        eys = sb.tile([P, 2, D], U8, name="eys", align_bytes=64)
+        gxr = sb.tile([P, 1, PACK], BF16, name="gxr", align_bytes=64)
+        gyr = sb.tile([P, 2, PACK], BF16, name="gyr", align_bytes=64)
+        gain = sb.tile([P, NB, PACK], F32, name="gain", align_bytes=64)
+        h_raw = tiles("h_raw", TILES, [P, D], BF16)
+        h_t = tiles("h_t", TILES, [P, D], BF16)
+        h_codes = tiles("h_codes", TILES, [P, KP * P], U32)
+        h_scales = tiles("h_scales", TILES, [P, KP * P], U8)
+        negmax = tiles("negmax", TILES, [P, NB], F32)
+        negmax_y = tiles("negmax_y", TILES, [P, 1], F32)
+        sums = tiles("sums", TILES, [P, 4], F32)
+        recips = tiles("recips", TILES, [P, 2], F32)
+        expo = tiles("expo", TILES, [P, NB * BANK], F32)
+        c_t = tiles("c_t", TILES, [P, NB * BANK], BF16)
+        c_codes = tiles("c_codes", TILES, [P, NB * P], U32)
+        c_scales = tiles("c_scales", TILES, [P, NB * P], U8)
+        res = tiles("res", 2, [P, PACK, D], F32)
+        res_b = tiles("res_b", 2, [P, D * PACK], BF16)
+        res_codes = tiles("res_codes", 2, [P, D], U32)
+        res_scales = tiles("res_scales", 2, [P, D], U8)
+
+        h_rows = h.rearrange("(g p t) k -> g t p k", g=2, t=PACK)
+        out_rows = out_0.rearrange("(g p t) m -> g t p m", g=2, t=PACK)
+        out_words = out_1.rearrange("g p m t -> g p (m t)").bitcast(I32)
+        out_scales = out_2.bitcast(I32)
+
+        def load_words(tile, words):
+            nc.sync.dma_start(out=tile[:].bitcast(I32), in_=words.bitcast(I32).rearrange("g p n -> p g n"))
+
+        def load_scales(engine, plane, scales):
+            rows = scales.bitcast(I32).rearrange("g q n -> q g n")
+            for quad in range(4):
+                engine.dma_start(out=plane[32 * quad : 32 * quad + 4].bitcast(I32), in_=rows[4 * quad : 4 * quad + 4])
+
+        def load_h(i):
+            nc.sync.dma_start(out=h_raw[i][:], in_=h_rows[i // PACK, i % PACK])
+
+        def turn_h(i, bank):
+            words = h_raw[i][:].bitcast(F32)
+            for kp in range(KP):
+                for u in range(2):
+                    q = 2 * kp + u
+                    nc.tensor.transpose(bank[:, P * q : P * (q + 1)], words[:, 256 * kp + u : 256 * (kp + 1) : 2], ident[:])
+
+        def copy_h(i, bank):
+            nc.scalar.copy(
+                out=h_t[i][:].bitcast(F32).rearrange("p (k r u) -> p k r u", k=KP, u=2),
+                in_=bank[:].rearrange("p (k u r) -> p k r u", k=KP, u=2),
+            )
+
+        def quant_h(i):
+            nc.vector.quantize_mx(out=h_codes[i][:].bitcast(FP8X4), scales=h_scales[i][:], in_=h_t[i][:])
+
+        def logits(i, j, bank):
+            for kp in range(KP):
+                if j == 0:
+                    w, s = wxw[:, kp, :], wxs[:, kp, :]
+                else:
+                    w = wyw[:, kp, 2 * BANK * (j - 1) : 2 * BANK * j]
+                    s = wys[:, kp, BANK * (j - 1) : BANK * j]
+                nc.tensor.matmul_mx(
+                    out=bank[:],
+                    lhsT=h_codes[i][:, P * kp : P * (kp + 1)].bitcast(FP8X4),
+                    lhsT_scale=h_scales[i][:, P * kp : P * (kp + 1)],
+                    rhs=w.bitcast(FP4X4),
+                    rhs_scale=s,
+                    start=(kp == 0),
+                    stop=(kp == KP - 1),
+                )
+
+        def row_max(i, j, bank):
+            nc.vector.tensor_reduce(out=negmax[i][:, j : j + 1], in_=bank[:], axis=AX.X, op=ALU.max, negate=True)
+
+        def join_max(i):
+            nc.gpsimd.tensor_scalar(
+                out=negmax_y[i][:], in0=negmax[i][:, 1:2], scalar1=negmax[i][:, 2:3], scalar2=LOWEST, op0=ALU.min, op1=ALU.max
+            )
+
+        def exp(i, j, bank):
+            col = (2, 0, 1)[j]
+            nc.scalar.activation(
+                out=expo[i][:, BANK * j : BANK * (j + 1)].rearrange("p (t q) -> p t q", t=PACK),
+                in_=bank[:].rearrange("p (q t) -> p t q", t=PACK),
+                func=ACT.Exp,
+                bias=negmax[i][:, 0:1] if j == 0 else negmax_y[i][:],
+                scale=1.0,
+                accum_out=sums[i][:, col : col + 1],
+            )
+
+        def join_sum(i):
+            nc.gpsimd.tensor_tensor(out=sums[i][:, 3:4], in0=sums[i][:, 0:1], in1=sums[i][:, 1:2], op=ALU.add)
+
+        def recip(i):
+            nc.vector.reciprocal(out=recips[i][:], in_=sums[i][:, 2:4])
+
+        def center(engine, i, j):
+            cols = expo[i][:, BANK * j : BANK * (j + 1)]
+            side = min(j, 1)
+            engine.tensor_scalar(
+                out=cols, in0=cols, scalar1=recips[i][:, side : side + 1], scalar2=-1.0 / (BX, BY)[side], op0=ALU.mult, op1=ALU.add
+            )
+
+        def turn_c(i, j, bank):
+            for t in range(PACK):
+                c0 = BANK * j + P * t
+                nc.tensor.transpose(bank[:, P * t : P * (t + 1)], expo[i][:, c0 : c0 + P], ident[:])
+
+        def gain_c(i, j, bank):
+            nc.vector.tensor_tensor(
+                out=c_t[i][:, BANK * j : BANK * (j + 1)].rearrange("p (r t) -> p r t", t=PACK),
+                in0=bank[:].rearrange("p (t r) -> p r t", t=PACK),
+                in1=gain[:, j : j + 1, :].to_broadcast([P, P, PACK]),
+                op=ALU.mult,
+            )
+
+        def quant_c(i, j):
+            nc.vector.quantize_mx(
+                out=c_codes[i][:, P * j : P * (j + 1)].bitcast(FP8X4),
+                scales=c_scales[i][:, P * j : P * (j + 1)],
+                in_=c_t[i][:, BANK * j : BANK * (j + 1)],
+            )
+
+        def embed_pass(i, half, j, bank):
+            words, plane, g = (exw, exs, 0) if j == 0 else (eyw, eys, j - 1)
+            nc.tensor.matmul_mx(
+                out=bank[:],
+                lhsT=c_codes[i][:, P * j : P * (j + 1)].bitcast(FP8X4),
+                lhsT_scale=c_scales[i][:, P * j : P * (j + 1)],
+                rhs=words[:, g, 2 * BANK * half : 2 * BANK * (half + 1)].bitcast(FP4X4),
+                rhs_scale=plane[:, g, BANK * half : BANK * (half + 1)],
+                start=(j == 0),
+                stop=(j == NB - 1),
+            )
+
+        def embed(i, half, bank):
+            for j in range(NB):
+                embed_pass(i, half, j, bank)
+
+        def copy_out(i, half, bank, lo=0, hi=BANK):
+            nc.scalar.copy(out=res[i // PACK][:, i % PACK, BANK * half + lo : BANK * half + hi], in_=bank[:, lo:hi])
+
+        def store_out(i, lo=0, hi=D):
+            g, t = divmod(i, PACK)
+            nc.sync.dma_start(out=out_rows[g, t][:, lo:hi], in_=res[g][:, t, lo:hi])
+
+        def weave(on_vector, g, lo, hi):
+            dst = res_b[g][:, PACK * lo : PACK * hi].rearrange("p (m t) -> p m t", t=PACK)
+            src = res[g][:, :, lo:hi].rearrange("p t m -> p m t")
+            if on_vector:
+                nc.vector.tensor_copy(out=dst, in_=src)
+            else:
+                nc.scalar.copy(out=dst, in_=src)
+
+        def quant_out(g, lo, hi):
+            nc.vector.quantize_mx(
+                out=res_codes[g][:, lo:hi].bitcast(FP8X4), scales=res_scales[g][:, lo:hi], in_=res_b[g][:, PACK * lo : PACK * hi]
+            )
+
+        def store_words(g, lo, hi):
+            nc.sync.dma_start(out=out_words[g][:, lo:hi], in_=res_codes[g][:, lo:hi].bitcast(I32))
+
+        def store_scales(g, engines):
+            for quad in range(4):
+                engines[quad].dma_start(
+                    out=out_scales[g][4 * quad : 4 * quad + 4], in_=res_scales[g][32 * quad : 32 * quad + 4].bitcast(I32)
+                )
+
+        load_h(0)
+        for plane in (wxs, wys):
+            nc.vector.memset(plane[:].bitcast(I32), 0)
+        nc.vector.memset(warm[:], 0.0)
+        nc.scalar.activation(out=warm2[:], in_=warm[:], func=ACT.Exp)
+        for plane in (exs, eys):
+            nc.vector.memset(plane[:].bitcast(I32), 0)
+        make_identity(nc, ident[:])
+        load_scales(nc.sync, wxs, wx_scales)
+        load_scales(nc.gpsimd, wys, wy_scales)
+        load_words(wxw, wx_words)
+        load_h(1)
+        load_words(wyw, wy_words)
+        load_h(2)
+        load_h(3)
+        nc.sync.dma_start(out=gxr[:], in_=gx.rearrange("(j p t) -> p j t", p=P, t=PACK))
+        nc.sync.dma_start(out=gyr[:], in_=gy.rearrange("(j p t) -> p j t", p=P, t=PACK))
+        load_scales(nc.sync, exs, ex_scales)
+        load_scales(nc.sync, eys, ey_scales)
+        load_words(exw, ex_words)
+        load_words(eyw, ey_words)
+        for i in range(4, TILES):
+            load_h(i)
+
+        a0, a1, a2, c0, c1 = banks[0], banks[1], banks[2], banks[6], banks[7]
+        ring = banks[3:6]
+        turns = []
+
+        def next_turn_bank():
+            turns.append(0)
+            return ring[(len(turns) - 1) % 3]
+
+        def logit_banks(i):
+            return (a0, a1, a2) if i == 0 else (c0, c1, a0) if i == 1 else (a1, a2, a0)
+
+        for i in range(2):
+            bank = next_turn_bank()
+            turn_h(i, bank)
+            copy_h(i, bank)
+            quant_h(i)
+
+        for s in range(-2, TILES - 2):
+            new, mid, old, ahead = s + 2, s + 1, s, s + 4
+            lb = logit_banks(new)
+            if mid >= 0:
+                for j in range(NB):
+                    center(nc.gpsimd, mid, j)
+            for j in range(NB):
+                logits(new, j, lb[j])
+                row_max(new, j, lb[j])
+            if old >= 1:
+                copy_out(old - 1, 1, c1)
+                store_out(old - 1)
+            if old >= PACK:
+                weave(False, 0, 256 * (old - PACK), 256 * (old - PACK) + 128)
+            exp(new, 0, lb[0])
+            if old >= PACK:
+                weave(False, 0, 256 * (old - PACK) + 128, 256 * (old - PACK) + 256)
+            join_max(new)
+            exp(new, 1, lb[1])
+            exp(new, 2, lb[2])
+            join_sum(new)
+            if s == -2:
+                nc.gpsimd.tensor_scalar(out=gain[:, 0:1, :], in0=gxr[:], scalar1=float(BX), scalar2=0.0, op0=ALU.mult, op1=ALU.add)
+                nc.gpsimd.tensor_scalar(out=gain[:, 1:3, :], in0=gyr[:], scalar1=float(BY), scalar2=0.0, op0=ALU.mult, op1=ALU.add)
+            if mid >= 0:
+                for j in range(NB):
+                    bank = next_turn_bank()
+                    turn_c(mid, j, bank)
+                    gain_c(mid, j, bank)
+            if ahead < TILES:
+                bank = next_turn_bank()
+                turn_h(ahead, bank)
+                copy_h(ahead, bank)
+            if mid >= 0:
+                for j in range(NB):
+                    quant_c(mid, j)
+            if ahead < TILES:
+                quant_h(ahead)
+            if old >= PACK:
+                quant_out(0, 256 * (old - PACK), 256 * (old - PACK) + 256)
+            recip(new)
+            if old >= 0:
+                embed(old, 0, c0)
+                embed(old, 1, c1)
+                copy_out(old, 0, c0)
+
+        last = TILES - 1
+        for j in range(NB):
+            center(nc.vector, last, j)
+        copy_out(last - 2, 1, c1)
+        store_out(last - 2)
+        embed(last - 1, 0, c0)
+        tb = [next_turn_bank() for j in range(NB)]
+        for j in range(NB):
+            turn_c(last, j, tb[j])
+        embed(last - 1, 1, c1)
+        weave(False, 0, 512, 640)
+        copy_out(last - 1, 0, c0)
+        weave(False, 0, 640, 896)
+        copy_out(last - 1, 1, c1)
+        store_out(last - 1)
+        weave(False, 0, 896, 1024)
+        gain_c(last, 0, tb[0])
+        gain_c(last, 1, tb[1])
+        quant_c(last, 0)
+        gain_c(last, 2, tb[2])
+        quant_c(last, 1)
+        quant_c(last, 2)
+        quant_out(0, 512, 1024)
+        store_words(0, 0, D)
+        store_scales(0, [nc.sync] * 4)
+        for j in range(NB):
+            embed_pass(last, 0, j, a1)
+            embed_pass(last, 1, j, a2)
+        for c in range(4):
+            copy_out(last, c // 2, (a1, a2)[c // 2], 256 * (c % 2), 256 * (c % 2) + 256)
+            if c % 2 == 1:
+                store_out(last, BANK * (c // 2), BANK * (c // 2 + 1))
+        weave(False, 1, 768, 1024)
+        weave(True, 1, 0, 256)
+        weave(True, 1, 256, 512)
+        quant_out(1, 0, 256)
+        weave(True, 1, 512, 768)
+        quant_out(1, 256, 512)
+        store_words(1, 0, 512)
+        quant_out(1, 768, 1024)
+        quant_out(1, 512, 768)
+        store_words(1, 512, 1024)
+        store_scales(1, [nc.scalar, nc.sync, nc.scalar, nc.sync])

@@ -23,7 +23,6 @@ BANK = 512
 TILES = R // P
 KP = D // BANK
 NB = (BX + BY) // BANK
-LOWEST = -3.0e38
 
 
 def tile_simccsoftcoordinatereembedding_x2_kernel(
@@ -58,7 +57,7 @@ def tile_simccsoftcoordinatereembedding_x2_kernel(
         h_codes = tiles("h_codes", TILES, [P, KP * P], U32)
         h_scales = tiles("h_scales", TILES, [P, KP * P], U8)
         negmax = tiles("negmax", TILES, [P, NB], F32)
-        negmax_y = tiles("negmax_y", TILES, [P, 1], F32)
+        neg_logits = tiles("neg_logits", TILES, [P, BANK], F32)
         sums = tiles("sums", TILES, [P, 4], F32)
         recips = tiles("recips", TILES, [P, 2], F32)
         expo = tiles("expo", TILES, [P, NB * BANK], F32)
@@ -120,33 +119,35 @@ def tile_simccsoftcoordinatereembedding_x2_kernel(
                 )
 
         def row_max(i, j, bank):
-            nc.vector.tensor_reduce(out=negmax[i][:, j : j + 1], in_=bank[:], axis=AX.X, op=ALU.max, negate=True)
-
-        def join_max(i):
-            nc.gpsimd.tensor_scalar(
-                out=negmax_y[i][:], in0=negmax[i][:, 1:2], scalar1=negmax[i][:, 2:3], scalar2=LOWEST, op0=ALU.min, op1=ALU.max
-            )
+            if j < 2:
+                nc.vector.tensor_reduce(out=negmax[i][:, j : j + 1], in_=bank[:], axis=AX.X, op=ALU.max, negate=True)
+            else:
+                nc.vector.tensor_scalar(
+                    out=neg_logits[i][:], in0=bank[:], scalar1=-1.0, scalar2=negmax[i][:, 1:2], op0=ALU.mult, op1=ALU.min,
+                    accum_out=negmax[i][:, 2:3],
+                )
 
         def exp(i, j, bank):
             col = (2, 0, 1)[j]
             nc.scalar.activation(
                 out=expo[i][:, BANK * j : BANK * (j + 1)].rearrange("p (t q) -> p t q", t=PACK),
-                in_=bank[:].rearrange("p (q t) -> p t q", t=PACK),
+                in_=(bank if j < 2 else neg_logits[i])[:].rearrange("p (q t) -> p t q", t=PACK),
                 func=ACT.Exp,
-                bias=negmax[i][:, 0:1] if j == 0 else negmax_y[i][:],
-                scale=1.0,
+                bias=negmax[i][:, 0:1] if j == 0 else negmax[i][:, 2:3],
+                scale=1.0 if j < 2 else -1.0,
                 accum_out=sums[i][:, col : col + 1],
             )
 
         def join_sum(i):
-            nc.gpsimd.tensor_tensor(out=sums[i][:, 3:4], in0=sums[i][:, 0:1], in1=sums[i][:, 1:2], op=ALU.add)
+            nc.vector.tensor_scalar(
+                out=sums[i][:, 3:4], in0=sums[i][:, 0:1], scalar1=sums[i][:, 1:2], scalar2=None, op0=ALU.add
+            )
 
         def recip(i):
             nc.vector.reciprocal(out=recips[i][:], in_=sums[i][:, 2:4])
 
-        def center(engine, i, j):
-            cols = expo[i][:, BANK * j : BANK * (j + 1)]
-            side = min(j, 1)
+        def center(engine, i, side):
+            cols = expo[i][:, 0:BX] if side == 0 else expo[i][:, BX : BX + BY]
             engine.tensor_scalar(
                 out=cols, in0=cols, scalar1=recips[i][:, side : side + 1], scalar2=-1.0 / (BX, BY)[side], op0=ALU.mult, op1=ALU.add
             )
@@ -194,9 +195,24 @@ def tile_simccsoftcoordinatereembedding_x2_kernel(
             g, t = divmod(i, PACK)
             nc.sync.dma_start(out=out_rows[g, t][:, lo:hi], in_=res[g][:, t, lo:hi])
 
+        def weave_gpsimd(g, lo, hi):
+            nc.gpsimd.tensor_scalar(
+                out=res_b[g][:, PACK * lo : PACK * hi].rearrange("p (m t) -> p m t", t=PACK),
+                in0=res[g][:, :, lo:hi].rearrange("p t m -> p m t"),
+                scalar1=1.0, scalar2=0.0, op0=ALU.mult, op1=ALU.add,
+            )
+
         def weave(on_vector, g, lo, hi):
             dst = res_b[g][:, PACK * lo : PACK * hi].rearrange("p (m t) -> p m t", t=PACK)
             src = res[g][:, :, lo:hi].rearrange("p t m -> p m t")
+            if on_vector:
+                nc.vector.tensor_copy(out=dst, in_=src)
+            else:
+                nc.scalar.copy(out=dst, in_=src)
+
+        def weave_pair(on_vector, g, u, lo, hi):
+            dst = res_b[g][:, PACK * lo : PACK * hi].rearrange("p (m t) -> p m t", t=PACK)[:, :, 2 * u : 2 * u + 2]
+            src = res[g][:, 2 * u : 2 * u + 2, lo:hi].rearrange("p t m -> p m t")
             if on_vector:
                 nc.vector.tensor_copy(out=dst, in_=src)
             else:
@@ -221,24 +237,24 @@ def tile_simccsoftcoordinatereembedding_x2_kernel(
             nc.vector.memset(plane[:].bitcast(I32), 0)
         nc.vector.memset(warm[:], 0.0)
         nc.scalar.activation(out=warm2[:], in_=warm[:], func=ACT.Exp)
-        for plane in (exs, eys):
-            nc.vector.memset(plane[:].bitcast(I32), 0)
         make_identity(nc, ident[:])
         load_scales(nc.sync, wxs, wx_scales)
-        load_scales(nc.gpsimd, wys, wy_scales)
         load_words(wxw, wx_words)
         load_h(1)
         load_words(wyw, wy_words)
-        load_h(2)
-        load_h(3)
+        load_scales(nc.sync, wys, wy_scales)
+        for plane in (exs, eys):
+            nc.vector.memset(plane[:].bitcast(I32), 0)
+        for i in range(2, 6):
+            load_h(i)
         nc.sync.dma_start(out=gxr[:], in_=gx.rearrange("(j p t) -> p j t", p=P, t=PACK))
         nc.sync.dma_start(out=gyr[:], in_=gy.rearrange("(j p t) -> p j t", p=P, t=PACK))
+        load_h(6)
+        load_h(7)
         load_scales(nc.sync, exs, ex_scales)
         load_scales(nc.sync, eys, ey_scales)
         load_words(exw, ex_words)
         load_words(eyw, ey_words)
-        for i in range(4, TILES):
-            load_h(i)
 
         a0, a1, a2, c0, c1 = banks[0], banks[1], banks[2], banks[6], banks[7]
         ring = banks[3:6]
@@ -249,100 +265,159 @@ def tile_simccsoftcoordinatereembedding_x2_kernel(
             return ring[(len(turns) - 1) % 3]
 
         def logit_banks(i):
-            return (a0, a1, a2) if i == 0 else (c0, c1, a0) if i == 1 else (a1, a2, a0)
+            return (c1, c0, a2) if i == 1 else (a1, a0, a2)
 
         for i in range(2):
             bank = next_turn_bank()
             turn_h(i, bank)
             copy_h(i, bank)
-            quant_h(i)
+        quant_h(0)
+        nc.gpsimd.tensor_scalar(out=gain[:, 0:1, :], in0=gxr[:], scalar1=float(BX), scalar2=0.0, op0=ALU.mult, op1=ALU.add)
+        nc.gpsimd.tensor_scalar(out=gain[:, 1:3, :], in0=gyr[:], scalar1=float(BY), scalar2=0.0, op0=ALU.mult, op1=ALU.add)
 
-        for s in range(-2, TILES - 2):
-            new, mid, old, ahead = s + 2, s + 1, s, s + 4
-            lb = logit_banks(new)
-            if mid >= 0:
-                for j in range(NB):
-                    center(nc.gpsimd, mid, j)
+        def turn_h_next(i):
+            bank = next_turn_bank()
+            turn_h(i, bank)
+            return bank
+
+        def turn_gain(i):
             for j in range(NB):
-                logits(new, j, lb[j])
-                row_max(new, j, lb[j])
+                bank = next_turn_bank()
+                turn_c(i, j, bank)
+                gain_c(i, j, bank)
+
+        def center_both(i):
+            center(nc.gpsimd, i, 0)
+            center(nc.gpsimd, i, 1)
+
+        lb = logit_banks(0)
+        for j in range(NB):
+            logits(0, j, lb[j])
+        b2 = turn_h_next(2)
+        b3 = turn_h_next(3)
+        row_max(0, 0, lb[0])
+        quant_h(1)
+        row_max(0, 1, lb[1])
+        exp(0, 0, lb[0])
+        copy_h(2, b2)
+        row_max(0, 2, lb[2])
+        quant_h(2)
+        exp(0, 1, lb[1])
+        exp(0, 2, lb[2])
+        copy_h(3, b3)
+        lb = logit_banks(1)
+        for j in (1, 0, 2):
+            logits(1, j, lb[j])
+        b4 = turn_h_next(4)
+        b5 = turn_h_next(5)
+        row_max(1, 1, lb[1])
+        row_max(1, 0, lb[0])
+        join_sum(0)
+        row_max(1, 2, lb[2])
+        recip(0)
+        center_both(0)
+        for j in range(NB):
+            exp(1, j, lb[j])
+        copy_h(4, b4)
+        copy_h(5, b5)
+        lb = logit_banks(2)
+        for j in (1, 0, 2):
+            logits(2, j, lb[j])
+        row_max(2, 1, lb[1])
+        join_sum(1)
+        row_max(2, 0, lb[0])
+        recip(1)
+        row_max(2, 2, lb[2])
+        quant_h(3)
+        center_both(1)
+        for j in range(NB):
+            exp(2, j, lb[j])
+        turn_gain(0)
+        turn_h(6, c0)
+        copy_h(6, c0)
+        for j in range(NB):
+            quant_c(0, j)
+        join_sum(2)
+        quant_h(4)
+        recip(2)
+
+        for s in range(3, TILES):
+            mid, old = s - 2, s - 3
+            lb = logit_banks(s)
+            center_both(s - 1)
+            for j in (1, 0, 2):
+                logits(s, j, lb[j])
+                row_max(s, j, lb[j])
             if old >= 1:
                 copy_out(old - 1, 1, c1)
                 store_out(old - 1)
-            if old >= PACK:
-                weave(False, 0, 256 * (old - PACK), 256 * (old - PACK) + 128)
-            exp(new, 0, lb[0])
-            if old >= PACK:
-                weave(False, 0, 256 * (old - PACK) + 128, 256 * (old - PACK) + 256)
-            join_max(new)
-            exp(new, 1, lb[1])
-            exp(new, 2, lb[2])
-            join_sum(new)
-            if s == -2:
-                nc.gpsimd.tensor_scalar(out=gain[:, 0:1, :], in0=gxr[:], scalar1=float(BX), scalar2=0.0, op0=ALU.mult, op1=ALU.add)
-                nc.gpsimd.tensor_scalar(out=gain[:, 1:3, :], in0=gyr[:], scalar1=float(BY), scalar2=0.0, op0=ALU.mult, op1=ALU.add)
-            if mid >= 0:
-                for j in range(NB):
-                    bank = next_turn_bank()
-                    turn_c(mid, j, bank)
-                    gain_c(mid, j, bank)
-            if ahead < TILES:
-                bank = next_turn_bank()
-                turn_h(ahead, bank)
-                copy_h(ahead, bank)
-            if mid >= 0:
-                for j in range(NB):
-                    quant_c(mid, j)
-            if ahead < TILES:
-                quant_h(ahead)
-            if old >= PACK:
-                quant_out(0, 256 * (old - PACK), 256 * (old - PACK) + 256)
-            recip(new)
-            if old >= 0:
-                embed(old, 0, c0)
-                embed(old, 1, c1)
-                copy_out(old, 0, c0)
+            if old == PACK:
+                weave(False, 0, 0, 256)
+                weave_gpsimd(0, 256, 512)
+            exp(s, 0, lb[0])
+            if s == 3:
+                turn_h(7, c1)
+                copy_h(7, c1)
+            exp(s, 1, lb[1])
+            exp(s, 2, lb[2])
+            turn_gain(mid)
+            for j in range(NB):
+                quant_c(mid, j)
+            join_sum(s)
+            if s + 2 < TILES:
+                quant_h(s + 2)
+            if s == TILES - 1:
+                quant_out(0, 0, 256)
+            recip(s)
+            embed(old, 0, c0)
+            embed(old, 1, c1)
+            copy_out(old, 0, c0)
 
         last = TILES - 1
+        center_both(last)
+        copy_out(4, 1, c1)
+        store_out(4)
+        weave(False, 0, 512, 768)
+        turn_gain(6)
         for j in range(NB):
-            center(nc.vector, last, j)
-        copy_out(last - 2, 1, c1)
-        store_out(last - 2)
-        embed(last - 1, 0, c0)
-        tb = [next_turn_bank() for j in range(NB)]
+            quant_c(6, j)
+        embed(5, 0, a0)
+        embed(5, 1, a1)
+        copy_out(5, 0, a0)
+        store_out(5, 0, BANK)
+        quant_out(0, 256, 768)
+        store_words(0, 0, 768)
+        weave(False, 0, 768, 1024)
+        copy_out(5, 1, a1)
+        store_out(5, BANK, D)
+        turn_gain(7)
         for j in range(NB):
-            turn_c(last, j, tb[j])
-        embed(last - 1, 1, c1)
-        weave(False, 0, 512, 640)
-        copy_out(last - 1, 0, c0)
-        weave(False, 0, 640, 896)
-        copy_out(last - 1, 1, c1)
-        store_out(last - 1)
-        weave(False, 0, 896, 1024)
-        gain_c(last, 0, tb[0])
-        gain_c(last, 1, tb[1])
-        quant_c(last, 0)
-        gain_c(last, 2, tb[2])
-        quant_c(last, 1)
-        quant_c(last, 2)
-        quant_out(0, 512, 1024)
-        store_words(0, 0, D)
+            quant_c(7, j)
+        quant_out(0, 768, 1024)
+        weave_pair(False, 1, 0, 0, 256)
+        embed(6, 0, c0)
+        embed(6, 1, c1)
+        copy_out(6, 0, c0)
+        store_out(6, 0, BANK)
+        store_words(0, 768, D)
         store_scales(0, [nc.sync] * 4)
-        for j in range(NB):
-            embed_pass(last, 0, j, a1)
-            embed_pass(last, 1, j, a2)
+        weave_pair(True, 1, 0, 256, 1024)
+        copy_out(6, 1, c1)
+        store_out(6, BANK, D)
+        embed(7, 0, a0)
+        embed(7, 1, a1)
         for c in range(4):
-            copy_out(last, c // 2, (a1, a2)[c // 2], 256 * (c % 2), 256 * (c % 2) + 256)
+            copy_out(last, c // 2, (a0, a1)[c // 2], 256 * (c % 2), 256 * (c % 2) + 256)
             if c % 2 == 1:
                 store_out(last, BANK * (c // 2), BANK * (c // 2 + 1))
-        weave(False, 1, 768, 1024)
-        weave(True, 1, 0, 256)
-        weave(True, 1, 256, 512)
+        weave_pair(False, 1, 1, 768, 1024)
+        weave_pair(True, 1, 1, 0, 256)
+        weave_pair(True, 1, 1, 256, 512)
         quant_out(1, 0, 256)
-        weave(True, 1, 512, 768)
+        weave_pair(True, 1, 1, 512, 768)
         quant_out(1, 256, 512)
         store_words(1, 0, 512)
-        quant_out(1, 768, 1024)
         quant_out(1, 512, 768)
+        quant_out(1, 768, 1024)
         store_words(1, 512, 1024)
         store_scales(1, [nc.scalar, nc.sync, nc.scalar, nc.sync])

@@ -23,6 +23,8 @@ BANK = 512
 TILES = R // P
 KP = D // BANK
 NB = (BX + BY) // BANK
+WARM = 4
+EARLY_GAIN = (2, 3, 4, 5)
 
 
 def tile_simccsoftcoordinatereembedding_x2_kernel(
@@ -49,30 +51,34 @@ def tile_simccsoftcoordinatereembedding_x2_kernel(
         eyw = sb.tile([P, 2, 2 * D], U8, name="eyw", align_bytes=64)
         exs = sb.tile([P, 1, D], U8, name="exs", align_bytes=64)
         eys = sb.tile([P, 2, D], U8, name="eys", align_bytes=64)
-        gxr = sb.tile([P, 1, PACK], BF16, name="gxr", align_bytes=64)
+        gxr = sb.tile([P, BX], BF16, name="gxr", align_bytes=64)
+        gain_x = sb.tile([P, BX], F32, name="gain_x", align_bytes=64)
+        zeros = sb.tile([P, BANK], BF16, name="zeros", align_bytes=64)
         gyr = sb.tile([P, 2, PACK], BF16, name="gyr", align_bytes=64)
+        gxp = sb.tile([P, 1, PACK], BF16, name="gxp", align_bytes=64)
         gain = sb.tile([P, NB, PACK], F32, name="gain", align_bytes=64)
         h_raw = tiles("h_raw", TILES, [P, D], BF16)
         h_t = tiles("h_t", TILES, [P, D], BF16)
         h_codes = tiles("h_codes", TILES, [P, KP * P], U32)
         h_scales = tiles("h_scales", TILES, [P, KP * P], U8)
         negmax = tiles("negmax", TILES, [P, NB], F32)
-        neg_logits = tiles("neg_logits", TILES, [P, BANK], F32)
-        sums = tiles("sums", TILES, [P, 4], F32)
+        neg_logits = tiles("neg_logits", 2, [P, BY], F32) * 4
+        c_x = tiles("c_x", TILES, [P, BX], BF16)
+        sums = tiles("sums", TILES, [P, 2], F32)
         recips = tiles("recips", TILES, [P, 2], F32)
-        expo = tiles("expo", TILES, [P, NB * BANK], F32)
+        expo = tiles("expo", 4, [P, NB * BANK], F32) * 2
         c_t = tiles("c_t", TILES, [P, NB * BANK], BF16)
         c_codes = tiles("c_codes", TILES, [P, NB * P], U32)
         c_scales = tiles("c_scales", TILES, [P, NB * P], U8)
         res = tiles("res", 2, [P, PACK, D], F32)
         res_b = tiles("res_b", 2, [P, D * PACK], BF16)
         res_codes = tiles("res_codes", 2, [P, D], U32)
-        res_scales = tiles("res_scales", 2, [P, D], U8)
+        res_scales = sb.tile([P, 2, D], U8, name="res_scales", align_bytes=64)
 
         h_rows = h.rearrange("(g p t) k -> g t p k", g=2, t=PACK)
         out_rows = out_0.rearrange("(g p t) m -> g t p m", g=2, t=PACK)
         out_words = out_1.rearrange("g p m t -> g p (m t)").bitcast(I32)
-        out_scales = out_2.bitcast(I32)
+        out_scales = out_2.bitcast(I32).rearrange("g q n -> q g n")
 
         def load_words(tile, words):
             nc.sync.dma_start(out=tile[:].bitcast(I32), in_=words.bitcast(I32).rearrange("g p n -> p g n"))
@@ -85,21 +91,27 @@ def tile_simccsoftcoordinatereembedding_x2_kernel(
         def load_h(i):
             nc.sync.dma_start(out=h_raw[i][:], in_=h_rows[i // PACK, i % PACK])
 
-        def turn_h(i, bank):
+        def turn_h(i, bank, passes=range(KP)):
             words = h_raw[i][:].bitcast(F32)
-            for kp in range(KP):
+            for kp in passes:
                 for u in range(2):
                     q = 2 * kp + u
                     nc.tensor.transpose(bank[:, P * q : P * (q + 1)], words[:, 256 * kp + u : 256 * (kp + 1) : 2], ident[:])
 
-        def copy_h(i, bank):
-            nc.scalar.copy(
-                out=h_t[i][:].bitcast(F32).rearrange("p (k r u) -> p k r u", k=KP, u=2),
-                in_=bank[:].rearrange("p (k u r) -> p k r u", k=KP, u=2),
-            )
+        def copy_h(i, bank, lo=0, hi=KP, on_vector=False):
+            dst = h_t[i][:].bitcast(F32)[:, 256 * lo : 256 * hi].rearrange("p (k r u) -> p k r u", r=P, u=2)
+            src = bank[:, 256 * lo : 256 * hi].rearrange("p (k u r) -> p k r u", r=P, u=2)
+            if on_vector:
+                nc.vector.tensor_copy(out=dst, in_=src)
+            else:
+                nc.scalar.copy(out=dst, in_=src)
 
-        def quant_h(i):
-            nc.vector.quantize_mx(out=h_codes[i][:].bitcast(FP8X4), scales=h_scales[i][:], in_=h_t[i][:])
+        def quant_h(i, lo=0, hi=KP):
+            nc.vector.quantize_mx(
+                out=h_codes[i][:, P * lo : P * hi].bitcast(FP8X4),
+                scales=h_scales[i][:, P * lo : P * hi],
+                in_=h_t[i][:, BANK * lo : BANK * hi],
+            )
 
         def logits(i, j, bank):
             for kp in range(KP):
@@ -119,37 +131,65 @@ def tile_simccsoftcoordinatereembedding_x2_kernel(
                 )
 
         def row_max(i, j, bank):
-            if j < 2:
-                nc.vector.tensor_reduce(out=negmax[i][:, j : j + 1], in_=bank[:], axis=AX.X, op=ALU.max, negate=True)
+            if j == 0:
+                nc.vector.tensor_reduce(out=negmax[i][:, 0:1], in_=bank[:], axis=AX.X, op=ALU.max, negate=True)
             else:
                 nc.vector.tensor_scalar(
-                    out=neg_logits[i][:], in0=bank[:], scalar1=-1.0, scalar2=negmax[i][:, 1:2], op0=ALU.mult, op1=ALU.min,
-                    accum_out=negmax[i][:, 2:3],
+                    out=neg_logits[i][:, BANK * (j - 1) : BANK * j].rearrange("p (t q) -> p t q", t=PACK),
+                    in0=bank[:].rearrange("p (q t) -> p t q", t=PACK),
+                    scalar1=-1.0,
+                    scalar2=None if j == 1 else negmax[i][:, 1:2],
+                    op0=ALU.mult,
+                    op1=ALU.min,
+                    accum_out=negmax[i][:, j : j + 1],
                 )
 
-        def exp(i, j, bank):
-            col = (2, 0, 1)[j]
+        def exp_x(i, bank):
+            e = 2 if i in EARLY_GAIN else 1
             nc.scalar.activation(
-                out=expo[i][:, BANK * j : BANK * (j + 1)].rearrange("p (t q) -> p t q", t=PACK),
-                in_=(bank if j < 2 else neg_logits[i])[:].rearrange("p (q t) -> p t q", t=PACK),
+                out=expo[i][:, 0:BX].rearrange("p (u q e) -> p u q e", q=P, e=e),
+                in_=bank[:].rearrange("p (q u e) -> p u q e", q=P, e=e),
                 func=ACT.Exp,
-                bias=negmax[i][:, 0:1] if j == 0 else negmax[i][:, 2:3],
-                scale=1.0 if j < 2 else -1.0,
-                accum_out=sums[i][:, col : col + 1],
+                bias=negmax[i][:, 0:1],
+                scale=1.0,
+                accum_out=sums[i][:, 0:1],
             )
 
-        def join_sum(i):
-            nc.vector.tensor_scalar(
-                out=sums[i][:, 3:4], in0=sums[i][:, 0:1], scalar1=sums[i][:, 1:2], scalar2=None, op0=ALU.add
+        def exp_y(i):
+            nc.scalar.activation(
+                out=expo[i][:, BX : BX + BY],
+                in_=neg_logits[i][:],
+                func=ACT.Exp,
+                bias=negmax[i][:, 2:3],
+                scale=-1.0,
+                accum_out=sums[i][:, 1:2],
             )
 
         def recip(i):
-            nc.vector.reciprocal(out=recips[i][:], in_=sums[i][:, 2:4])
+            nc.vector.reciprocal(out=recips[i][:], in_=sums[i][:])
 
         def center(engine, i, side):
             cols = expo[i][:, 0:BX] if side == 0 else expo[i][:, BX : BX + BY]
             engine.tensor_scalar(
                 out=cols, in0=cols, scalar1=recips[i][:, side : side + 1], scalar2=-1.0 / (BX, BY)[side], op0=ALU.mult, op1=ALU.add
+            )
+
+        def center_x_scalar(i):
+            cols = expo[i][:, 0:BX]
+            nc.scalar.activation(out=cols, in_=cols, func=ACT.Copy, bias=-1.0 / BX, scale=recips[i][:, 0:1])
+
+        def gain_cx(i):
+            nc.gpsimd.tensor_tensor(out=c_x[i][:], in0=expo[i][:, 0:BX], in1=gain_x[:], op=ALU.mult)
+
+        def turn_cx(i, bank):
+            words = c_x[i][:].bitcast(F32)
+            for u in range(2):
+                nc.tensor.transpose(bank[:, P * u : P * (u + 1)], words[:, P * u : P * (u + 1)], ident[:])
+
+        def copy_cx(i, bank):
+            nc.scalar.copy(
+                out=c_t[i][:, 0:BX].bitcast(F32).rearrange("p (r u) -> p r u", u=2),
+                in_=bank[:, 0 : 2 * P].rearrange("p (u r) -> p r u", u=2),
             )
 
         def turn_c(i, j, bank):
@@ -165,11 +205,11 @@ def tile_simccsoftcoordinatereembedding_x2_kernel(
                 op=ALU.mult,
             )
 
-        def quant_c(i, j):
+        def quant_c(i, lo, hi):
             nc.vector.quantize_mx(
-                out=c_codes[i][:, P * j : P * (j + 1)].bitcast(FP8X4),
-                scales=c_scales[i][:, P * j : P * (j + 1)],
-                in_=c_t[i][:, BANK * j : BANK * (j + 1)],
+                out=c_codes[i][:, P * lo : P * hi].bitcast(FP8X4),
+                scales=c_scales[i][:, P * lo : P * hi],
+                in_=c_t[i][:, BANK * lo : BANK * hi],
             )
 
         def embed_pass(i, half, j, bank):
@@ -180,12 +220,12 @@ def tile_simccsoftcoordinatereembedding_x2_kernel(
                 lhsT_scale=c_scales[i][:, P * j : P * (j + 1)],
                 rhs=words[:, g, 2 * BANK * half : 2 * BANK * (half + 1)].bitcast(FP4X4),
                 rhs_scale=plane[:, g, BANK * half : BANK * (half + 1)],
-                start=(j == 0),
-                stop=(j == NB - 1),
+                start=(j == 1),
+                stop=(j == 0),
             )
 
         def embed(i, half, bank):
-            for j in range(NB):
+            for j in (1, 2, 0):
                 embed_pass(i, half, j, bank)
 
         def copy_out(i, half, bank, lo=0, hi=BANK):
@@ -220,204 +260,219 @@ def tile_simccsoftcoordinatereembedding_x2_kernel(
 
         def quant_out(g, lo, hi):
             nc.vector.quantize_mx(
-                out=res_codes[g][:, lo:hi].bitcast(FP8X4), scales=res_scales[g][:, lo:hi], in_=res_b[g][:, PACK * lo : PACK * hi]
+                out=res_codes[g][:, lo:hi].bitcast(FP8X4), scales=res_scales[:, g, lo:hi], in_=res_b[g][:, PACK * lo : PACK * hi]
             )
 
         def store_words(g, lo, hi):
             nc.sync.dma_start(out=out_words[g][:, lo:hi], in_=res_codes[g][:, lo:hi].bitcast(I32))
 
-        def store_scales(g, engines):
+        def store_scales(engines):
             for quad in range(4):
                 engines[quad].dma_start(
-                    out=out_scales[g][4 * quad : 4 * quad + 4], in_=res_scales[g][32 * quad : 32 * quad + 4].bitcast(I32)
+                    out=out_scales[4 * quad : 4 * quad + 4], in_=res_scales[32 * quad : 32 * quad + 4].bitcast(I32)
                 )
 
+        a0, a1, a2, b0, b1, b2, c0, c1 = banks
         load_h(0)
-        for plane in (wxs, wys):
-            nc.vector.memset(plane[:].bitcast(I32), 0)
+        nc.vector.memset(wxs[:].bitcast(I32), 0)
+        nc.vector.memset(zeros[:], 0.0)
+        nc.vector.memset(wys[:].bitcast(I32), 0)
         nc.vector.memset(warm[:], 0.0)
         nc.scalar.activation(out=warm2[:], in_=warm[:], func=ACT.Exp)
         make_identity(nc, ident[:])
+        for n in range(WARM):
+            nc.tensor.matmul(c1[:], zeros[:, 0:P], zeros[:], start=True, stop=True)
         load_scales(nc.sync, wxs, wx_scales)
-        load_words(wxw, wx_words)
         load_h(1)
+        load_words(wxw, wx_words)
         load_words(wyw, wy_words)
         load_scales(nc.sync, wys, wy_scales)
+        for i in range(2, 5):
+            load_h(i)
+        nc.sync.dma_start(out=gxp[:], in_=gx.rearrange("(j p t) -> p j t", p=P, t=PACK))
+        nc.sync.dma_start(out=gyr[:], in_=gy.rearrange("(j p t) -> p j t", p=P, t=PACK))
+        nc.sync.dma_start(out=gxr[:], in_=gx.partition_broadcast(P))
+        for i in range(5, TILES):
+            load_h(i)
+
+        def on_gpsimd(i):
+            center(nc.gpsimd, i, 0)
+            center(nc.gpsimd, i, 1)
+            if i in EARLY_GAIN:
+                gain_cx(i)
+
+        def turn_all(i):
+            if i in EARLY_GAIN:
+                turn_cx(i, b2)
+            else:
+                turn_c(i, 0, b2)
+            turn_c(i, 1, b0)
+            turn_c(i, 2, b1)
+
+        nc.gpsimd.tensor_scalar(out=gain[:, 0:1, :], in0=gxp[:], scalar1=float(BX), scalar2=0.0, op0=ALU.mult, op1=ALU.add)
+        nc.gpsimd.tensor_scalar(out=gain[:, 1:3, :], in0=gyr[:], scalar1=float(BY), scalar2=0.0, op0=ALU.mult, op1=ALU.add)
+
+        turn_h(0, b0, (0,))
+        turn_h(0, b1, (1,))
+        turn_h(1, b2)
+        for n in range(2):
+            nc.tensor.matmul(c1[:], zeros[:, 0:P], zeros[:], start=True, stop=True)
+        copy_h(0, b0, 0, 1)
+        copy_h(0, b1, 1, 2, True)
+        quant_h(0, 0, 1)
+        quant_h(0, 1, 2)
+        copy_h(1, b2)
+        logits(0, 0, a1)
+        logits(0, 1, a0)
+        logits(0, 2, a2)
+        turn_h(2, b0)
+        quant_h(1)
         for plane in (exs, eys):
             nc.vector.memset(plane[:].bitcast(I32), 0)
-        for i in range(2, 6):
-            load_h(i)
-        nc.sync.dma_start(out=gxr[:], in_=gx.rearrange("(j p t) -> p j t", p=P, t=PACK))
-        nc.sync.dma_start(out=gyr[:], in_=gy.rearrange("(j p t) -> p j t", p=P, t=PACK))
-        load_h(6)
-        load_h(7)
         load_scales(nc.sync, exs, ex_scales)
         load_scales(nc.sync, eys, ey_scales)
         load_words(exw, ex_words)
         load_words(eyw, ey_words)
-
-        a0, a1, a2, c0, c1 = banks[0], banks[1], banks[2], banks[6], banks[7]
-        ring = banks[3:6]
-        turns = []
-
-        def next_turn_bank():
-            turns.append(0)
-            return ring[(len(turns) - 1) % 3]
-
-        def logit_banks(i):
-            return (c1, c0, a2) if i == 1 else (a1, a0, a2)
-
-        for i in range(2):
-            bank = next_turn_bank()
-            turn_h(i, bank)
-            copy_h(i, bank)
-        quant_h(0)
-        nc.gpsimd.tensor_scalar(out=gain[:, 0:1, :], in0=gxr[:], scalar1=float(BX), scalar2=0.0, op0=ALU.mult, op1=ALU.add)
-        nc.gpsimd.tensor_scalar(out=gain[:, 1:3, :], in0=gyr[:], scalar1=float(BY), scalar2=0.0, op0=ALU.mult, op1=ALU.add)
-
-        def turn_h_next(i):
-            bank = next_turn_bank()
-            turn_h(i, bank)
-            return bank
-
-        def turn_gain(i):
-            for j in range(NB):
-                bank = next_turn_bank()
-                turn_c(i, j, bank)
-                gain_c(i, j, bank)
-
-        def center_both(i):
-            center(nc.gpsimd, i, 0)
-            center(nc.gpsimd, i, 1)
-
-        lb = logit_banks(0)
-        for j in range(NB):
-            logits(0, j, lb[j])
-        b2 = turn_h_next(2)
-        b3 = turn_h_next(3)
-        row_max(0, 0, lb[0])
-        quant_h(1)
-        row_max(0, 1, lb[1])
-        exp(0, 0, lb[0])
-        copy_h(2, b2)
-        row_max(0, 2, lb[2])
+        row_max(0, 0, a1)
+        row_max(0, 1, a0)
+        exp_x(0, a1)
+        copy_h(2, b0)
+        row_max(0, 2, a2)
+        exp_y(0)
+        logits(1, 1, c0)
+        logits(1, 0, c1)
+        logits(1, 2, a0)
+        turn_h(3, b1)
+        turn_h(4, b2)
+        row_max(1, 1, c0)
         quant_h(2)
-        exp(0, 1, lb[1])
-        exp(0, 2, lb[2])
-        copy_h(3, b3)
-        lb = logit_banks(1)
-        for j in (1, 0, 2):
-            logits(1, j, lb[j])
-        b4 = turn_h_next(4)
-        b5 = turn_h_next(5)
-        row_max(1, 1, lb[1])
-        row_max(1, 0, lb[0])
-        join_sum(0)
-        row_max(1, 2, lb[2])
+        row_max(1, 0, c1)
         recip(0)
-        center_both(0)
-        for j in range(NB):
-            exp(1, j, lb[j])
-        copy_h(4, b4)
-        copy_h(5, b5)
-        lb = logit_banks(2)
-        for j in (1, 0, 2):
-            logits(2, j, lb[j])
-        row_max(2, 1, lb[1])
-        join_sum(1)
-        row_max(2, 0, lb[0])
-        recip(1)
-        row_max(2, 2, lb[2])
+        row_max(1, 2, a0)
+        nc.gpsimd.tensor_scalar(
+            out=gain_x[:].rearrange("p (u q e) -> p u q e", u=2, e=2),
+            in0=gxr[:].rearrange("p (q u e) -> p u q e", u=2, e=2),
+            scalar1=float(BX), scalar2=0.0, op0=ALU.mult, op1=ALU.add,
+        )
+        on_gpsimd(0)
+        exp_x(1, c1)
+        exp_y(1)
+        copy_h(3, b1, 0, KP, True)
+        copy_h(4, b2)
+        logits(2, 1, a2)
+        logits(2, 0, a1)
+        logits(2, 2, a0)
+        row_max(2, 1, a2)
+        row_max(2, 0, a1)
         quant_h(3)
-        center_both(1)
-        for j in range(NB):
-            exp(2, j, lb[j])
-        turn_gain(0)
-        turn_h(6, c0)
-        copy_h(6, c0)
-        for j in range(NB):
-            quant_c(0, j)
-        join_sum(2)
+        recip(1)
+        on_gpsimd(1)
+        row_max(2, 2, a0)
+        exp_x(2, a1)
+        exp_y(2)
+        turn_c(0, 1, b0)
+        turn_c(0, 2, b1)
+        turn_c(0, 0, b2)
+        turn_h(5, c0)
+        gain_c(0, 1, b0)
+        gain_c(0, 2, b1)
+        gain_c(0, 0, b2)
+        copy_h(5, c0)
         quant_h(4)
+        quant_c(0, 1, 3)
+        quant_c(0, 0, 1)
         recip(2)
 
         for s in range(3, TILES):
             mid, old = s - 2, s - 3
-            lb = logit_banks(s)
-            center_both(s - 1)
-            for j in (1, 0, 2):
-                logits(s, j, lb[j])
-                row_max(s, j, lb[j])
+            on_gpsimd(s - 1)
+            for j, bank in ((1, a2), (0, a1), (2, a0)):
+                logits(s, j, bank)
+                row_max(s, j, bank)
             if old >= 1:
                 copy_out(old - 1, 1, c1)
                 store_out(old - 1)
-            if old == PACK:
-                weave(False, 0, 0, 256)
-                weave_gpsimd(0, 256, 512)
-            exp(s, 0, lb[0])
-            if s == 3:
-                turn_h(7, c1)
-                copy_h(7, c1)
-            exp(s, 1, lb[1])
-            exp(s, 2, lb[2])
-            turn_gain(mid)
-            for j in range(NB):
-                quant_c(mid, j)
-            join_sum(s)
+            if s in (5, 6):
+                weave_pair(False, 0, 0, 384 * (s - 5), 384 * (s - 4))
+            if s == 7:
+                weave_gpsimd(0, 768, 1024)
+                weave_pair(False, 0, 1, 0, 384)
+            exp_x(s, a1)
+            if s in (3, 4):
+                turn_h(s + 3, c1)
+                copy_h(s + 3, c1)
+            turn_all(mid)
+            if mid in EARLY_GAIN:
+                copy_cx(mid, b2)
+            else:
+                gain_c(mid, 0, b2)
+            exp_y(s)
+            gain_c(mid, 1, b0)
+            gain_c(mid, 2, b1)
+            quant_c(mid, 0, 1)
             if s + 2 < TILES:
                 quant_h(s + 2)
             if s == TILES - 1:
                 quant_out(0, 0, 256)
+                store_words(0, 0, 256)
+            quant_c(mid, 1, 3)
             recip(s)
             embed(old, 0, c0)
             embed(old, 1, c1)
             copy_out(old, 0, c0)
 
-        last = TILES - 1
-        center_both(last)
+        center(nc.gpsimd, 7, 1)
+        turn_all(6)
+        gain_c(6, 0, b2)
+        center_x_scalar(7)
         copy_out(4, 1, c1)
         store_out(4)
-        weave(False, 0, 512, 768)
-        turn_gain(6)
-        for j in range(NB):
-            quant_c(6, j)
+        gain_c(6, 1, b0)
+        gain_c(6, 2, b1)
+        weave_pair(False, 0, 1, 384, 768)
+        quant_c(6, 0, 1)
+        quant_c(6, 1, 3)
         embed(5, 0, a0)
-        embed(5, 1, a1)
         copy_out(5, 0, a0)
         store_out(5, 0, BANK)
-        quant_out(0, 256, 768)
-        store_words(0, 0, 768)
-        weave(False, 0, 768, 1024)
+        weave_pair(False, 1, 0, 0, 256)
+        turn_c(7, 1, b0)
+        turn_c(7, 2, b1)
+        turn_c(7, 0, b2)
+        gain_c(7, 1, b0)
+        gain_c(7, 2, b1)
+        gain_c(7, 0, b2)
+        quant_c(7, 1, 3)
+        quant_c(7, 0, 1)
+        embed(5, 1, a1)
+        embed(6, 0, a2)
+        embed(7, 0, c0)
+        embed(6, 1, c1)
+        embed(7, 1, a0)
         copy_out(5, 1, a1)
         store_out(5, BANK, D)
-        turn_gain(7)
-        for j in range(NB):
-            quant_c(7, j)
+        quant_out(0, 256, 768)
         quant_out(0, 768, 1024)
-        weave_pair(False, 1, 0, 0, 256)
-        embed(6, 0, c0)
-        embed(6, 1, c1)
-        copy_out(6, 0, c0)
+        copy_out(6, 0, a2)
         store_out(6, 0, BANK)
-        store_words(0, 768, D)
-        store_scales(0, [nc.sync] * 4)
-        weave_pair(True, 1, 0, 256, 1024)
+        store_words(0, 256, D)
+        weave_pair(False, 1, 0, 896, 1024)
+        weave_pair(True, 1, 0, 256, 768)
+        copy_out(7, 0, c0)
+        store_out(7, 0, BANK)
+        weave_pair(True, 1, 1, 0, 512)
         copy_out(6, 1, c1)
         store_out(6, BANK, D)
-        embed(7, 0, a0)
-        embed(7, 1, a1)
-        for c in range(4):
-            copy_out(last, c // 2, (a0, a1)[c // 2], 256 * (c % 2), 256 * (c % 2) + 256)
-            if c % 2 == 1:
-                store_out(last, BANK * (c // 2), BANK * (c // 2 + 1))
-        weave_pair(False, 1, 1, 768, 1024)
-        weave_pair(True, 1, 1, 0, 256)
-        weave_pair(True, 1, 1, 256, 512)
-        quant_out(1, 0, 256)
-        weave_pair(True, 1, 1, 512, 768)
-        quant_out(1, 256, 512)
+        weave_pair(True, 1, 0, 768, 896)
+        quant_out(1, 0, 512)
         store_words(1, 0, 512)
+        copy_out(7, 1, a0, 0, 256)
+        copy_out(7, 1, a0, 256, 512)
+        store_out(7, BANK, D)
+        weave_pair(True, 1, 1, 512, 768)
+        weave_pair(True, 1, 1, 768, 896)
+        weave_pair(False, 1, 1, 896, 1024)
         quant_out(1, 512, 768)
         quant_out(1, 768, 1024)
         store_words(1, 512, 1024)
-        store_scales(1, [nc.scalar, nc.sync, nc.scalar, nc.sync])
+        store_scales([nc.scalar, nc.sync, nc.scalar, nc.sync])

@@ -258,6 +258,13 @@ def tile_simccsoftcoordinatereembedding_x2_kernel(
             else:
                 nc.scalar.copy(out=dst, in_=src)
 
+        def weave_pair_gpsimd(g, u, lo, hi):
+            nc.gpsimd.tensor_scalar(
+                out=res_b[g][:, PACK * lo : PACK * hi].rearrange("p (m t) -> p m t", t=PACK)[:, :, 2 * u : 2 * u + 2],
+                in0=res[g][:, 2 * u : 2 * u + 2, lo:hi].rearrange("p t m -> p m t"),
+                scalar1=1.0, scalar2=0.0, op0=ALU.mult, op1=ALU.add,
+            )
+
         def quant_out(g, lo, hi):
             nc.vector.quantize_mx(
                 out=res_codes[g][:, lo:hi].bitcast(FP8X4), scales=res_scales[:, g, lo:hi], in_=res_b[g][:, PACK * lo : PACK * hi]
@@ -274,26 +281,39 @@ def tile_simccsoftcoordinatereembedding_x2_kernel(
 
         a0, a1, a2, b0, b1, b2, c0, c1 = banks
         load_h(0)
-        nc.vector.memset(wxs[:].bitcast(I32), 0)
-        nc.vector.memset(zeros[:], 0.0)
         nc.vector.memset(wys[:].bitcast(I32), 0)
+        nc.vector.memset(zeros[:], 0.0)
+        nc.vector.memset(wxs[:].bitcast(I32), 0)
         nc.vector.memset(warm[:], 0.0)
         nc.scalar.activation(out=warm2[:], in_=warm[:], func=ACT.Exp)
         make_identity(nc, ident[:])
         for n in range(WARM):
             nc.tensor.matmul(c1[:], zeros[:, 0:P], zeros[:], start=True, stop=True)
-        load_scales(nc.sync, wxs, wx_scales)
         load_h(1)
-        load_words(wxw, wx_words)
-        load_words(wyw, wy_words)
         load_scales(nc.sync, wys, wy_scales)
-        for i in range(2, 5):
-            load_h(i)
+        load_words(wyw, wy_words)
+        load_words(wxw, wx_words)
+        load_scales(nc.sync, wxs, wx_scales)
+        load_h(2)
         nc.sync.dma_start(out=gxp[:], in_=gx.rearrange("(j p t) -> p j t", p=P, t=PACK))
+        load_h(3)
+        load_h(4)
         nc.sync.dma_start(out=gyr[:], in_=gy.rearrange("(j p t) -> p j t", p=P, t=PACK))
         nc.sync.dma_start(out=gxr[:], in_=gx.partition_broadcast(P))
         for i in range(5, TILES):
             load_h(i)
+
+        def turn_x(i):
+            if i in EARLY_GAIN:
+                turn_cx(i, b2)
+            else:
+                turn_c(i, 0, b2)
+
+        def empty_x(i):
+            if i in EARLY_GAIN:
+                copy_cx(i, b2)
+            else:
+                gain_c(i, 0, b2)
 
         def on_gpsimd(i):
             center(nc.gpsimd, i, 0)
@@ -310,43 +330,43 @@ def tile_simccsoftcoordinatereembedding_x2_kernel(
             turn_c(i, 2, b1)
 
         nc.gpsimd.tensor_scalar(out=gain[:, 0:1, :], in0=gxp[:], scalar1=float(BX), scalar2=0.0, op0=ALU.mult, op1=ALU.add)
+        nc.gpsimd.memset(exs[:].bitcast(I32), 0)
+        nc.gpsimd.memset(eys[:].bitcast(I32), 0)
         nc.gpsimd.tensor_scalar(out=gain[:, 1:3, :], in0=gyr[:], scalar1=float(BY), scalar2=0.0, op0=ALU.mult, op1=ALU.add)
 
         turn_h(0, b0, (0,))
         turn_h(0, b1, (1,))
         turn_h(1, b2)
-        for n in range(2):
+        for n in range(1):
             nc.tensor.matmul(c1[:], zeros[:, 0:P], zeros[:], start=True, stop=True)
         copy_h(0, b0, 0, 1)
         copy_h(0, b1, 1, 2, True)
         quant_h(0, 0, 1)
         quant_h(0, 1, 2)
         copy_h(1, b2)
-        logits(0, 0, a1)
         logits(0, 1, a0)
         logits(0, 2, a2)
-        turn_h(2, b0)
         quant_h(1)
-        for plane in (exs, eys):
-            nc.vector.memset(plane[:].bitcast(I32), 0)
+        logits(1, 1, c0)
+        logits(0, 0, a1)
+        turn_h(2, b0)
+        row_max(0, 1, a0)
+        row_max(0, 2, a2)
+        row_max(0, 0, a1)
         load_scales(nc.sync, exs, ex_scales)
         load_scales(nc.sync, eys, ey_scales)
         load_words(exw, ex_words)
         load_words(eyw, ey_words)
-        row_max(0, 0, a1)
-        row_max(0, 1, a0)
-        exp_x(0, a1)
-        copy_h(2, b0)
-        row_max(0, 2, a2)
         exp_y(0)
-        logits(1, 1, c0)
+        copy_h(2, b0)
+        exp_x(0, a1)
         logits(1, 0, c1)
         logits(1, 2, a0)
         turn_h(3, b1)
         turn_h(4, b2)
         row_max(1, 1, c0)
-        quant_h(2)
         row_max(1, 0, c1)
+        quant_h(2)
         recip(0)
         row_max(1, 2, a0)
         nc.gpsimd.tensor_scalar(
@@ -354,10 +374,11 @@ def tile_simccsoftcoordinatereembedding_x2_kernel(
             in0=gxr[:].rearrange("p (q u e) -> p u q e", u=2, e=2),
             scalar1=float(BX), scalar2=0.0, op0=ALU.mult, op1=ALU.add,
         )
-        on_gpsimd(0)
+        center(nc.gpsimd, 0, 1)
+        center(nc.gpsimd, 0, 0)
         exp_x(1, c1)
+        copy_h(3, b1)
         exp_y(1)
-        copy_h(3, b1, 0, KP, True)
         copy_h(4, b2)
         logits(2, 1, a2)
         logits(2, 0, a1)
@@ -370,24 +391,28 @@ def tile_simccsoftcoordinatereembedding_x2_kernel(
         row_max(2, 2, a0)
         exp_x(2, a1)
         exp_y(2)
+        turn_h(5, c0)
         turn_c(0, 1, b0)
         turn_c(0, 2, b1)
+        logits(3, 1, a2)
         turn_c(0, 0, b2)
-        turn_h(5, c0)
+        turn_h(6, c1)
         gain_c(0, 1, b0)
         gain_c(0, 2, b1)
         gain_c(0, 0, b2)
         copy_h(5, c0)
+        copy_h(6, c1)
         quant_h(4)
         quant_c(0, 1, 3)
-        quant_c(0, 0, 1)
         recip(2)
+        quant_c(0, 0, 1)
 
         for s in range(3, TILES):
             mid, old = s - 2, s - 3
             on_gpsimd(s - 1)
             for j, bank in ((1, a2), (0, a1), (2, a0)):
-                logits(s, j, bank)
+                if (s, j) != (3, 1):
+                    logits(s, j, bank)
                 row_max(s, j, bank)
             if old >= 1:
                 copy_out(old - 1, 1, c1)
@@ -397,10 +422,10 @@ def tile_simccsoftcoordinatereembedding_x2_kernel(
             if s == 7:
                 weave_gpsimd(0, 768, 1024)
                 weave_pair(False, 0, 1, 0, 384)
+            if s == 4:
+                turn_h(7, c1)
+                copy_h(7, c1)
             exp_x(s, a1)
-            if s in (3, 4):
-                turn_h(s + 3, c1)
-                copy_h(s + 3, c1)
             turn_all(mid)
             if mid in EARLY_GAIN:
                 copy_cx(mid, b2)
@@ -415,33 +440,44 @@ def tile_simccsoftcoordinatereembedding_x2_kernel(
             if s == TILES - 1:
                 quant_out(0, 0, 256)
                 store_words(0, 0, 256)
-            quant_c(mid, 1, 3)
-            recip(s)
+            if s < TILES - 1:
+                recip(s)
+                quant_c(mid, 1, 3)
+            else:
+                quant_c(mid, 1, 3)
+                recip(s)
             embed(old, 0, c0)
+            if s == TILES - 1:
+                turn_c(6, 1, b0)
+                turn_c(6, 0, b2)
+                turn_c(6, 2, b1)
             embed(old, 1, c1)
             copy_out(old, 0, c0)
 
         center(nc.gpsimd, 7, 1)
-        turn_all(6)
-        gain_c(6, 0, b2)
         center_x_scalar(7)
+        if 7 in EARLY_GAIN:
+            gain_cx(7)
         copy_out(4, 1, c1)
         store_out(4)
         gain_c(6, 1, b0)
+        gain_c(6, 0, b2)
         gain_c(6, 2, b1)
-        weave_pair(False, 0, 1, 384, 768)
         quant_c(6, 0, 1)
         quant_c(6, 1, 3)
         embed(5, 0, a0)
         copy_out(5, 0, a0)
         store_out(5, 0, BANK)
-        weave_pair(False, 1, 0, 0, 256)
+        weave_pair_gpsimd(1, 0, 0, 256)
+        weave_pair_gpsimd(0, 1, 640, 768)
+        weave_pair(False, 0, 1, 384, 640)
+        weave_pair(False, 1, 0, 256, 512)
         turn_c(7, 1, b0)
         turn_c(7, 2, b1)
-        turn_c(7, 0, b2)
+        turn_x(7)
         gain_c(7, 1, b0)
         gain_c(7, 2, b1)
-        gain_c(7, 0, b2)
+        empty_x(7)
         quant_c(7, 1, 3)
         quant_c(7, 0, 1)
         embed(5, 1, a1)
@@ -456,14 +492,13 @@ def tile_simccsoftcoordinatereembedding_x2_kernel(
         copy_out(6, 0, a2)
         store_out(6, 0, BANK)
         store_words(0, 256, D)
-        weave_pair(False, 1, 0, 896, 1024)
-        weave_pair(True, 1, 0, 256, 768)
+        weave_pair(True, 1, 0, 512, 896)
         copy_out(7, 0, c0)
         store_out(7, 0, BANK)
         weave_pair(True, 1, 1, 0, 512)
         copy_out(6, 1, c1)
         store_out(6, BANK, D)
-        weave_pair(True, 1, 0, 768, 896)
+        weave_pair(False, 1, 0, 896, 1024)
         quant_out(1, 0, 512)
         store_words(1, 0, 512)
         copy_out(7, 1, a0, 0, 256)

from contextlib import ExitStack

import concourse.mybir as mybir
from concourse.masks import make_identity

R, D, BX, BY = 1024, 1024, 512, 1024
FLOPS = 2 * R * D * (BX + BY) * 2

F32 = mybir.dt.float32
BF16 = mybir.dt.bfloat16
I32 = mybir.dt.int32
U32 = mybir.dt.uint32
U8 = mybir.dt.uint8
FP8X4 = mybir.dt.float8_e4m3fn_x4
FP4X4 = mybir.dt.float4_e2m1fn_x4
ALU = mybir.AluOpType
ACT = mybir.ActivationFunctionType
AX = mybir.AxisListType

P = 128
PACK = 4
BANK = 512
TILES = R // P
KP = D // BANK
NB = (BX + BY) // BANK
WARM = 4
EARLY_GAIN = (2, 3, 4, 5)


def tile_simccsoftcoordinatereembedding_x2_kernel(
    tc, h, wx_words, wx_scales, wy_words, wy_scales, gx, gy, ex_words, ex_scales, ey_words, ey_scales, out_0, out_1, out_2
):
    nc = tc.nc
    with ExitStack() as ctx:
        sb = ctx.enter_context(tc.tile_pool(name="sb", bufs=1))
        ps = ctx.enter_context(tc.psum_pool(name="ps", bufs=1))
        ctx.enter_context(tc.manual_schedule())

        def tiles(name, count, shape, dtype):
            return [sb.tile(shape, dtype, name="%s%d" % (name, n), align_bytes=64) for n in range(count)]

        banks = [ps.tile([P, BANK], F32, name="bank%d" % n) for n in range(8)]
        ident = sb.tile([P, P], F32, name="ident", align_bytes=64)
        warm = sb.tile([P, 8], F32, name="warm", align_bytes=64)
        warm2 = sb.tile([P, 8], F32, name="warm2", align_bytes=64)
        wxw = sb.tile([P, KP, 2 * BX], U8, name="wxw", align_bytes=64)
        wyw = sb.tile([P, KP, 2 * BY], U8, name="wyw", align_bytes=64)
        wxs = sb.tile([P, KP, BX], U8, name="wxs", align_bytes=64)
        wys = sb.tile([P, KP, BY], U8, name="wys", align_bytes=64)
        exw = sb.tile([P, 1, 2 * D], U8, name="exw", align_bytes=64)
        eyw = sb.tile([P, 2, 2 * D], U8, name="eyw", align_bytes=64)
        exs = sb.tile([P, 1, D], U8, name="exs", align_bytes=64)
        eys = sb.tile([P, 2, D], U8, name="eys", align_bytes=64)
        gxr = sb.tile([P, BX], BF16, name="gxr", align_bytes=64)
        gain_x = sb.tile([P, BX], F32, name="gain_x", align_bytes=64)
        zeros = sb.tile([P, BANK], BF16, name="zeros", align_bytes=64)
        gyr = sb.tile([P, 2, PACK], BF16, name="gyr", align_bytes=64)
        gxp = sb.tile([P, 1, PACK], BF16, name="gxp", align_bytes=64)
        gain = sb.tile([P, NB, PACK], F32, name="gain", align_bytes=64)
        h_raw = tiles("h_raw", TILES, [P, D], BF16)
        h_t = tiles("h_t", TILES, [P, D], BF16)
        h_codes = tiles("h_codes", TILES, [P, KP * P], U32)
        h_scales = tiles("h_scales", TILES, [P, KP * P], U8)
        negmax = tiles("negmax", TILES, [P, NB], F32)
        neg_logits = tiles("neg_logits", 2, [P, BY], F32) * 4
        c_x = tiles("c_x", TILES, [P, BX], BF16)
        sums = tiles("sums", TILES, [P, 2], F32)
        recips = tiles("recips", TILES, [P, 2], F32)
        expo = tiles("expo", 4, [P, NB * BANK], F32) * 2
        c_t = tiles("c_t", TILES, [P, NB * BANK], BF16)
        c_codes = tiles("c_codes", TILES, [P, NB * P], U32)
        c_scales = tiles("c_scales", TILES, [P, NB * P], U8)
        res = tiles("res", 2, [P, PACK, D], F32)
        res_b = tiles("res_b", 2, [P, D * PACK], BF16)
        res_codes = tiles("res_codes", 2, [P, D], U32)
        res_scales = sb.tile([P, 2, D], U8, name="res_scales", align_bytes=64)

        h_rows = h.rearrange("(g p t) k -> g t p k", g=2, t=PACK)
        out_rows = out_0.rearrange("(g p t) m -> g t p m", g=2, t=PACK)
        out_words = out_1.rearrange("g p m t -> g p (m t)").bitcast(I32)
        out_scales = out_2.bitcast(I32).rearrange("g q n -> q g n")

        def load_words(tile, words):
            nc.sync.dma_start(out=tile[:].bitcast(I32), in_=words.bitcast(I32).rearrange("g p n -> p g n"))

        def load_scales(engine, plane, scales):
            rows = scales.bitcast(I32).rearrange("g q n -> q g n")
            for quad in range(4):
                engine.dma_start(out=plane[32 * quad : 32 * quad + 4].bitcast(I32), in_=rows[4 * quad : 4 * quad + 4])

        def load_h(i):
            nc.sync.dma_start(out=h_raw[i][:], in_=h_rows[i // PACK, i % PACK])

        def turn_h(i, bank, passes=range(KP)):
            words = h_raw[i][:].bitcast(F32)
            for kp in passes:
                for u in range(2):
                    q = 2 * kp + u
                    nc.tensor.transpose(bank[:, P * q : P * (q + 1)], words[:, 256 * kp + u : 256 * (kp + 1) : 2], ident[:])

        def copy_h(i, bank, lo=0, hi=KP, on_vector=False):
            dst = h_t[i][:].bitcast(F32)[:, 256 * lo : 256 * hi].rearrange("p (k r u) -> p k r u", r=P, u=2)
            src = bank[:, 256 * lo : 256 * hi].rearrange("p (k u r) -> p k r u", r=P, u=2)
            if on_vector:
                nc.vector.tensor_copy(out=dst, in_=src)
            else:
                nc.scalar.copy(out=dst, in_=src)

        def quant_h(i, lo=0, hi=KP):
            nc.vector.quantize_mx(
                out=h_codes[i][:, P * lo : P * hi].bitcast(FP8X4),
                scales=h_scales[i][:, P * lo : P * hi],
                in_=h_t[i][:, BANK * lo : BANK * hi],
            )

        def logits(i, j, bank):
            for kp in range(KP):
                if j == 0:
                    w, s = wxw[:, kp, :], wxs[:, kp, :]
                else:
                    w = wyw[:, kp, 2 * BANK * (j - 1) : 2 * BANK * j]
                    s = wys[:, kp, BANK * (j - 1) : BANK * j]
                nc.tensor.matmul_mx(
                    out=bank[:],
                    lhsT=h_codes[i][:, P * kp : P * (kp + 1)].bitcast(FP8X4),
                    lhsT_scale=h_scales[i][:, P * kp : P * (kp + 1)],
                    rhs=w.bitcast(FP4X4),
                    rhs_scale=s,
                    start=(kp == 0),
                    stop=(kp == KP - 1),
                )

        def row_max(i, j, bank):
            if j == 0:
                nc.vector.tensor_reduce(out=negmax[i][:, 0:1], in_=bank[:], axis=AX.X, op=ALU.max, negate=True)
            else:
                nc.vector.tensor_scalar(
                    out=neg_logits[i][:, BANK * (j - 1) : BANK * j].rearrange("p (t q) -> p t q", t=PACK),
                    in0=bank[:].rearrange("p (q t) -> p t q", t=PACK),
                    scalar1=-1.0,
                    scalar2=None if j == 1 else negmax[i][:, 1:2],
                    op0=ALU.mult,
                    op1=ALU.min,
                    accum_out=negmax[i][:, j : j + 1],
                )

        def exp_x(i, bank):
            e = 2 if i in EARLY_GAIN else 1
            nc.scalar.activation(
                out=expo[i][:, 0:BX].rearrange("p (u q e) -> p u q e", q=P, e=e),
                in_=bank[:].rearrange("p (q u e) -> p u q e", q=P, e=e),
                func=ACT.Exp,
                bias=negmax[i][:, 0:1],
                scale=1.0,
                accum_out=sums[i][:, 0:1],
            )

        def exp_y(i):
            nc.scalar.activation(
                out=expo[i][:, BX : BX + BY],
                in_=neg_logits[i][:],
                func=ACT.Exp,
                bias=negmax[i][:, 2:3],
                scale=-1.0,
                accum_out=sums[i][:, 1:2],
            )

        def recip(i):
            nc.vector.reciprocal(out=recips[i][:], in_=sums[i][:])

        def center(engine, i, side):
            cols = expo[i][:, 0:BX] if side == 0 else expo[i][:, BX : BX + BY]
            engine.tensor_scalar(
                out=cols, in0=cols, scalar1=recips[i][:, side : side + 1], scalar2=-1.0 / (BX, BY)[side], op0=ALU.mult, op1=ALU.add
            )

        def center_x_scalar(i):
            cols = expo[i][:, 0:BX]
            nc.scalar.activation(out=cols, in_=cols, func=ACT.Copy, bias=-1.0 / BX, scale=recips[i][:, 0:1])

        def gain_cx(i):
            nc.gpsimd.tensor_tensor(out=c_x[i][:], in0=expo[i][:, 0:BX], in1=gain_x[:], op=ALU.mult)

        def turn_cx(i, bank):
            words = c_x[i][:].bitcast(F32)
            for u in range(2):
                nc.tensor.transpose(bank[:, P * u : P * (u + 1)], words[:, P * u : P * (u + 1)], ident[:])

        def copy_cx(i, bank):
            nc.scalar.copy(
                out=c_t[i][:, 0:BX].bitcast(F32).rearrange("p (r u) -> p r u", u=2),
                in_=bank[:, 0 : 2 * P].rearrange("p (u r) -> p r u", u=2),
            )

        def turn_c(i, j, bank):
            for t in range(PACK):
                c0 = BANK * j + P * t
                nc.tensor.transpose(bank[:, P * t : P * (t + 1)], expo[i][:, c0 : c0 + P], ident[:])

        def gain_c(i, j, bank):
            nc.vector.tensor_tensor(
                out=c_t[i][:, BANK * j : BANK * (j + 1)].rearrange("p (r t) -> p r t", t=PACK),
                in0=bank[:].rearrange("p (t r) -> p r t", t=PACK),
                in1=gain[:, j : j + 1, :].to_broadcast([P, P, PACK]),
                op=ALU.mult,
            )

        def quant_c(i, lo, hi):
            nc.vector.quantize_mx(
                out=c_codes[i][:, P * lo : P * hi].bitcast(FP8X4),
                scales=c_scales[i][:, P * lo : P * hi],
                in_=c_t[i][:, BANK * lo : BANK * hi],
            )

        def embed_pass(i, half, j, bank):
            words, plane, g = (exw, exs, 0) if j == 0 else (eyw, eys, j - 1)
            nc.tensor.matmul_mx(
                out=bank[:],
                lhsT=c_codes[i][:, P * j : P * (j + 1)].bitcast(FP8X4),
                lhsT_scale=c_scales[i][:, P * j : P * (j + 1)],
                rhs=words[:, g, 2 * BANK * half : 2 * BANK * (half + 1)].bitcast(FP4X4),
                rhs_scale=plane[:, g, BANK * half : BANK * (half + 1)],
                start=(j == 1),
                stop=(j == 0),
            )

        def embed(i, half, bank):
            for j in (1, 2, 0):
                embed_pass(i, half, j, bank)

        def copy_out(i, half, bank, lo=0, hi=BANK):
            nc.scalar.copy(out=res[i // PACK][:, i % PACK, BANK * half + lo : BANK * half + hi], in_=bank[:, lo:hi])

        def store_out(i, lo=0, hi=D):
            g, t = divmod(i, PACK)
            nc.sync.dma_start(out=out_rows[g, t][:, lo:hi], in_=res[g][:, t, lo:hi])

        def weave_gpsimd(g, lo, hi):
            nc.gpsimd.tensor_scalar(
                out=res_b[g][:, PACK * lo : PACK * hi].rearrange("p (m t) -> p m t", t=PACK),
                in0=res[g][:, :, lo:hi].rearrange("p t m -> p m t"),
                scalar1=1.0, scalar2=0.0, op0=ALU.mult, op1=ALU.add,
            )

        def weave(on_vector, g, lo, hi):
            dst = res_b[g][:, PACK * lo : PACK * hi].rearrange("p (m t) -> p m t", t=PACK)
            src = res[g][:, :, lo:hi].rearrange("p t m -> p m t")
            if on_vector:
                nc.vector.tensor_copy(out=dst, in_=src)
            else:
                nc.scalar.copy(out=dst, in_=src)

        def weave_pair(on_vector, g, u, lo, hi):
            dst = res_b[g][:, PACK * lo : PACK * hi].rearrange("p (m t) -> p m t", t=PACK)[:, :, 2 * u : 2 * u + 2]
            src = res[g][:, 2 * u : 2 * u + 2, lo:hi].rearrange("p t m -> p m t")
            if on_vector:
                nc.vector.tensor_copy(out=dst, in_=src)
            else:
                nc.scalar.copy(out=dst, in_=src)

        def weave_pair_gpsimd(g, u, lo, hi):
            nc.gpsimd.tensor_scalar(
                out=res_b[g][:, PACK * lo : PACK * hi].rearrange("p (m t) -> p m t", t=PACK)[:, :, 2 * u : 2 * u + 2],
                in0=res[g][:, 2 * u : 2 * u + 2, lo:hi].rearrange("p t m -> p m t"),
                scalar1=1.0, scalar2=0.0, op0=ALU.mult, op1=ALU.add,
            )

        def quant_out(g, lo, hi):
            nc.vector.quantize_mx(
                out=res_codes[g][:, lo:hi].bitcast(FP8X4), scales=res_scales[:, g, lo:hi], in_=res_b[g][:, PACK * lo : PACK * hi]
            )

        def store_words(g, lo, hi):
            nc.sync.dma_start(out=out_words[g][:, lo:hi], in_=res_codes[g][:, lo:hi].bitcast(I32))

        def store_scales(engines):
            for quad in range(4):
                engines[quad].dma_start(
                    out=out_scales[4 * quad : 4 * quad + 4], in_=res_scales[32 * quad : 32 * quad + 4].bitcast(I32)
                )

        a0, a1, a2, b0, b1, b2, c0, c1 = banks
        load_h(0)
        nc.vector.memset(wys[:].bitcast(I32), 0)
        nc.vector.memset(zeros[:], 0.0)
        nc.vector.memset(wxs[:].bitcast(I32), 0)
        nc.vector.memset(warm[:], 0.0)
        nc.scalar.activation(out=warm2[:], in_=warm[:], func=ACT.Exp)
        make_identity(nc, ident[:])
        for n in range(WARM):
            nc.tensor.matmul(c1[:], zeros[:, 0:P], zeros[:], start=True, stop=True)
        load_h(1)
        load_scales(nc.sync, wys, wy_scales)
        load_words(wyw, wy_words)
        load_words(wxw, wx_words)
        load_scales(nc.sync, wxs, wx_scales)
        load_h(2)
        nc.sync.dma_start(out=gxp[:], in_=gx.rearrange("(j p t) -> p j t", p=P, t=PACK))
        load_h(3)
        load_h(4)
        nc.sync.dma_start(out=gyr[:], in_=gy.rearrange("(j p t) -> p j t", p=P, t=PACK))
        nc.sync.dma_start(out=gxr[:], in_=gx.partition_broadcast(P))
        for i in range(5, TILES):
            load_h(i)

        def turn_x(i):
            if i in EARLY_GAIN:
                turn_cx(i, b2)
            else:
                turn_c(i, 0, b2)

        def empty_x(i):
            if i in EARLY_GAIN:
                copy_cx(i, b2)
            else:
                gain_c(i, 0, b2)

        def on_gpsimd(i):
            center(nc.gpsimd, i, 0)
            center(nc.gpsimd, i, 1)
            if i in EARLY_GAIN:
                gain_cx(i)

        def turn_all(i):
            if i in EARLY_GAIN:
                turn_cx(i, b2)
            else:
                turn_c(i, 0, b2)
            turn_c(i, 1, b0)
            turn_c(i, 2, b1)

        nc.gpsimd.tensor_scalar(out=gain[:, 0:1, :], in0=gxp[:], scalar1=float(BX), scalar2=0.0, op0=ALU.mult, op1=ALU.add)
        nc.gpsimd.memset(exs[:].bitcast(I32), 0)
        nc.gpsimd.memset(eys[:].bitcast(I32), 0)
        nc.gpsimd.tensor_scalar(out=gain[:, 1:3, :], in0=gyr[:], scalar1=float(BY), scalar2=0.0, op0=ALU.mult, op1=ALU.add)

        turn_h(0, b0, (0,))
        turn_h(0, b1, (1,))
        turn_h(1, b2)
        for n in range(1):
            nc.tensor.matmul(c1[:], zeros[:, 0:P], zeros[:], start=True, stop=True)
        copy_h(0, b0, 0, 1)
        copy_h(0, b1, 1, 2, True)
        quant_h(0, 0, 1)
        quant_h(0, 1, 2)
        copy_h(1, b2)
        logits(0, 1, a0)
        logits(0, 2, a2)
        quant_h(1)
        logits(1, 1, c0)
        logits(0, 0, a1)
        turn_h(2, b0)
        row_max(0, 1, a0)
        row_max(0, 2, a2)
        row_max(0, 0, a1)
        load_scales(nc.sync, exs, ex_scales)
        load_scales(nc.sync, eys, ey_scales)
        load_words(exw, ex_words)
        load_words(eyw, ey_words)
        exp_y(0)
        copy_h(2, b0)
        exp_x(0, a1)
        logits(1, 0, c1)
        logits(1, 2, a0)
        turn_h(3, b1)
        turn_h(4, b2)
        row_max(1, 1, c0)
        row_max(1, 0, c1)
        quant_h(2)
        recip(0)
        row_max(1, 2, a0)
        nc.gpsimd.tensor_scalar(
            out=gain_x[:].rearrange("p (u q e) -> p u q e", u=2, e=2),
            in0=gxr[:].rearrange("p (q u e) -> p u q e", u=2, e=2),
            scalar1=float(BX), scalar2=0.0, op0=ALU.mult, op1=ALU.add,
        )
        center(nc.gpsimd, 0, 1)
        center(nc.gpsimd, 0, 0)
        exp_x(1, c1)
        copy_h(3, b1)
        exp_y(1)
        copy_h(4, b2)
        logits(2, 1, a2)
        logits(2, 0, a1)
        logits(2, 2, a0)
        row_max(2, 1, a2)
        row_max(2, 0, a1)
        quant_h(3)
        recip(1)
        on_gpsimd(1)
        row_max(2, 2, a0)
        exp_x(2, a1)
        exp_y(2)
        turn_h(5, c0)
        turn_c(0, 1, b0)
        turn_c(0, 2, b1)
        logits(3, 1, a2)
        turn_c(0, 0, b2)
        turn_h(6, c1)
        gain_c(0, 1, b0)
        gain_c(0, 2, b1)
        gain_c(0, 0, b2)
        copy_h(5, c0)
        copy_h(6, c1)
        quant_h(4)
        quant_c(0, 1, 3)
        recip(2)
        quant_c(0, 0, 1)

        for s in range(3, TILES):
            mid, old = s - 2, s - 3
            on_gpsimd(s - 1)
            for j, bank in ((1, a2), (0, a1), (2, a0)):
                if (s, j) != (3, 1):
                    logits(s, j, bank)
                row_max(s, j, bank)
            if old >= 1:
                copy_out(old - 1, 1, c1)
                store_out(old - 1)
            if s in (5, 6):
                weave_pair(False, 0, 0, 384 * (s - 5), 384 * (s - 4))
            if s == 7:
                weave_gpsimd(0, 768, 1024)
                weave_pair(False, 0, 1, 0, 384)
            if s == 4:
                turn_h(7, c1)
                copy_h(7, c1)
            exp_x(s, a1)
            turn_all(mid)
            if mid in EARLY_GAIN:
                copy_cx(mid, b2)
            else:
                gain_c(mid, 0, b2)
            exp_y(s)
            gain_c(mid, 1, b0)
            gain_c(mid, 2, b1)
            quant_c(mid, 0, 1)
            if s + 2 < TILES:
                quant_h(s + 2)
            if s == TILES - 1:
                quant_out(0, 0, 256)
                store_words(0, 0, 256)
            if s < TILES - 1:
                recip(s)
                quant_c(mid, 1, 3)
            else:
                quant_c(mid, 1, 3)
                recip(s)
            embed(old, 0, c0)
            if s == TILES - 1:
                turn_c(6, 1, b0)
                turn_c(6, 0, b2)
                turn_c(6, 2, b1)
            embed(old, 1, c1)
            copy_out(old, 0, c0)

        center(nc.gpsimd, 7, 1)
        center_x_scalar(7)
        if 7 in EARLY_GAIN:
            gain_cx(7)
        copy_out(4, 1, c1)
        store_out(4)
        gain_c(6, 1, b0)
        gain_c(6, 0, b2)
        gain_c(6, 2, b1)
        quant_c(6, 0, 1)
        quant_c(6, 1, 3)
        embed(5, 0, a0)
        copy_out(5, 0, a0)
        store_out(5, 0, BANK)
        weave_pair_gpsimd(1, 0, 0, 256)
        weave_pair_gpsimd(0, 1, 640, 768)
        weave_pair(False, 0, 1, 384, 640)
        weave_pair(False, 1, 0, 256, 512)
        turn_c(7, 1, b0)
        turn_c(7, 2, b1)
        turn_x(7)
        gain_c(7, 1, b0)
        gain_c(7, 2, b1)
        empty_x(7)
        quant_c(7, 1, 3)
        quant_c(7, 0, 1)
        embed(5, 1, a1)
        embed(6, 0, a2)
        embed(7, 0, c0)
        embed(6, 1, c1)
        embed(7, 1, a0)
        copy_out(5, 1, a1)
        store_out(5, BANK, D)
        quant_out(0, 256, 768)
        quant_out(0, 768, 1024)
        copy_out(6, 0, a2)
        store_out(6, 0, BANK)
        store_words(0, 256, D)
        weave_pair(True, 1, 0, 512, 896)
        copy_out(7, 0, c0)
        store_out(7, 0, BANK)
        weave_pair(True, 1, 1, 0, 512)
        copy_out(6, 1, c1)
        store_out(6, BANK, D)
        weave_pair(False, 1, 0, 896, 1024)
        quant_out(1, 0, 512)
        store_words(1, 0, 512)
        copy_out(7, 1, a0, 0, 256)
        copy_out(7, 1, a0, 256, 512)
        store_out(7, BANK, D)
        weave_pair(True, 1, 1, 512, 768)
        weave_pair(True, 1, 1, 768, 896)
        weave_pair(False, 1, 1, 896, 1024)
        quant_out(1, 512, 768)
        quant_out(1, 768, 1024)
        store_words(1, 512, 1024)
        store_scales([nc.scalar, nc.sync, nc.scalar, nc.sync])
